import numpy as np
import ml_dtypes


def mxq(x, axis, fmt="e4m3"):
    dtype, down = {"e4m3": (ml_dtypes.float8_e4m3fn, 7), "e5m2": (ml_dtypes.float8_e5m2, 14)}[fmt]
    v = np.moveaxis(np.asarray(x, np.float32).astype(ml_dtypes.bfloat16).astype(np.float64), axis, -1)
    blocks = v.reshape(v.shape[:-1] + (-1, 32))
    amax = np.abs(blocks).max(-1, keepdims=True)
    byte = np.maximum(np.where(amax > 0, np.frexp(amax)[1] - 1 + 127, 0) - down, 1)
    scale = np.exp2(byte - 127.0)
    codes = (blocks / scale).astype(np.float32).astype(dtype).astype(np.float64)
    return np.moveaxis((codes * scale).reshape(v.shape), -1, axis)


WIDE = False


def mx_kscale(k):
    if not WIDE:
        return np.ones(k)
    levels = np.array([10, -10, 5, -5, 0])
    if k % 512:
        return np.exp2(np.random.permutation(np.resize(levels, k // 32))).repeat(32)
    a = np.empty((k // 512, 16))
    for p in range(k // 512):
        a[p, :8] = np.random.permutation(np.resize(levels, 8))
        for g in range(8):
            far = levels[np.abs(levels - a[p, g]) >= 10]
            a[p, g + 8] = far[np.random.randint(len(far))]
    return np.exp2(a.ravel()).repeat(32)


def f64(x):
    return np.asarray(x).astype(np.float64)


def striped(idx):
    return np.tile(idx.reshape(-1, 16).T, (8, 1)).astype(np.uint16)


def unstriped(offs):
    return offs[:16].T.reshape(-1).astype(np.int64)


def striped8(idx):
    return np.concatenate([x.reshape(-1, 16).T for x in idx]).astype(np.uint16)


def runs(offs, k):
    lists = np.stack([offs[16 * r : 16 * r + 16].T.reshape(-1) for r in range(8)]).astype(np.int64)
    return lists[np.arange(k) % 512 // 64]


def pack_weight(w):
    k, n = w.shape
    w = f64(np.asarray(w, np.float32).astype(ml_dtypes.bfloat16)).reshape(k // 32, 32, n)
    amax = np.abs(w).max(1)
    byte = np.clip(np.where(amax > 0, np.frexp(amax)[1] - 1 + 127 - 7, 1), 1, 254)
    scaled = (w * np.exp2(127.0 - byte)[:, None, :]).reshape(k, n).astype(np.float32)
    words = np.ascontiguousarray(scaled.reshape(k // 512, 128, 4, n).transpose(0, 1, 3, 2)).astype(ml_dtypes.float8_e4m3fn).view(np.uint8)
    return words, np.ascontiguousarray(byte.astype(np.uint8).reshape(k // 512, 16, n))


def unpack_weight(words, scales):
    g, p, n, _ = words.shape
    vals = np.ascontiguousarray(words).view(ml_dtypes.float8_e4m3fn).astype(np.float64) * np.repeat(np.exp2(scales.astype(np.float64) - 127.0), 8, axis=1)[..., None]
    return vals.transpose(0, 1, 3, 2).reshape(g * 512, n)


def sigmoid(v):
    return 1.0 / (1.0 + np.exp(-np.maximum(v, -700.0)))


K, T, S, N, G, H = 512, 2048, 512, 512, 2048, 512


def setup_inputs():
    n = np.random.standard_normal
    s = mx_kscale(K)[:, None]
    u = mx_kscale(S)
    packed_xT = pack_weight(n((K, T)) * s)
    packed_dT = pack_weight(n((K, G)) / s)
    return {
        "x_words": packed_xT[0],
        "x_scales": packed_xT[1],
        "d_words": packed_dT[0],
        "d_scales": packed_dT[1],
        "gn": (np.random.uniform(0.5, 1.5, (H, 1)) * u[:, None]).astype(np.float32),
        "w1": (n((H, N)) / np.sqrt(H) / u[:, None]).astype(np.float32),
        "offs": striped(np.random.permutation(T)[:S]),
        "kidx": striped8(np.random.randint(0, G, (8, H))),
        "n1": striped8(np.stack([np.random.permutation(S) for _ in range(8)])),
        "n2": striped8(np.stack([np.random.permutation(S) for _ in range(8)])),
        "n3": striped8(np.stack([np.random.permutation(S) for _ in range(8)])),
    }


def reference(x_words, x_scales, d_words, d_scales, gn, w1, offs, kidx, n1, n2, n3):
    d_kidx = unpack_weight(d_words, d_scales)[np.arange(K)[:, None], runs(kidx, K)]
    xq = unpack_weight(x_words, x_scales)[:, unstriped(offs)]
    s = 0.0625 * (d_kidx.T @ xq)
    pa = s[np.arange(H)[:, None], runs(n1, H)]
    pb = s[np.arange(H)[:, None], runs(n2, H)]
    mu = 0.3125 * (s + pa + pb)
    z = f64(gn) * ((s - mu) / (np.sqrt((pa - mu) ** 2 + (pb - mu) ** 2 + 0.25)))
    h = mxq(f64(w1), 0, "e4m3").T @ mxq(z, 0, "e4m3")
    return h * (sigmoid(h[np.arange(N)[:, None], runs(n3, N)]))

@@ -1,0 +1,229 @@
+from contextlib import ExitStack
+
+import concourse.mybir as mybir
+from concourse.masks import make_identity
+
+F32 = mybir.dt.float32
+BF16 = mybir.dt.bfloat16
+I32 = mybir.dt.int32
+U32 = mybir.dt.uint32
+U16 = mybir.dt.uint16
+U8 = mybir.dt.uint8
+FP8X4 = mybir.dt.float8_e4m3fn_x4
+ACT = mybir.ActivationFunctionType
+ALU = mybir.AluOpType
+
+P = 128
+PACK = 4
+TABLE = 2048
+S = 512
+CHUNK = 128
+CHUNKS = S // CHUNK
+LIST_COLS = CHUNK // 16
+HALF = S // 2
+
+FLOPS = 2 * 2 * 512 * 512 * 512
+
+MU = 0.3125
+
+
+def tile_picked_keystdgate_none_p_kernel(
+    tc, x_words, x_scales, d_words, d_scales, gn, w1, offs, kidx, n1, n2, n3, out
+):
+    nc = tc.nc
+    with ExitStack() as ctx:
+        keep = ctx.enter_context(tc.tile_pool(name="keep", bufs=1))
+        psum = ctx.enter_context(tc.psum_pool(name="psum", bufs=1))
+
+        def sb(name, shape, dtype, tag=None):
+            return keep.tile(shape, dtype, name=name, tag=tag or name, align_bytes=64)
+
+        lists = {}
+        for name in ("kidx", "offs", "n1", "n2", "n3"):
+            lists[name] = keep.tile([P, S // 16], U16, name="list_" + name)
+
+        d_scale_table = sb("d_scale_table", [P, TABLE], U8)
+        x_scale_table = sb("x_scale_table", [P, TABLE], U8)
+        d_word_table = sb("d_word_table", [P, TABLE], U32)
+        x_word_table = sb("x_word_table", [P, TABLE], U32)
+        nc.vector.memset(d_scale_table[:].bitcast(I32), 0)
+        nc.gpsimd.memset(x_scale_table[:].bitcast(I32), 0)
+
+        warm = sb("warm", [P, 2], F32)
+        nc.vector.memset(warm[:, 0:1], 1.0)
+        nc.scalar.activation(warm[:, 1:2], warm[:, 0:1], ACT.Abs_reciprocal_sqrt)
+
+        nc.sync.dma_start(lists["kidx"][:], kidx)
+        for j in range(2):
+            nc.scalar.dma_start(d_scale_table[j:P:16, :].bitcast(I32), d_scales[0][j:16:2, :].bitcast(I32))
+        nc.sync.dma_start(d_word_table[:].bitcast(I32), d_words[0].rearrange("p n t -> p (n t)").bitcast(I32))
+        nc.sync.dma_start(lists["offs"][:], offs)
+        nc.sync.dma_start(x_word_table[:].bitcast(I32), x_words[0].rearrange("p n t -> p (n t)").bitcast(I32))
+        for q in range(4):
+            nc.gpsimd.dma_start(
+                x_scale_table[32 * q : 32 * q + 4, :].bitcast(I32), x_scales[0][4 * q : 4 * q + 4, :].bitcast(I32)
+            )
+        nc.sync.dma_start(lists["n1"][:], n1)
+        nc.sync.dma_start(lists["n2"][:], n2)
+        nc.sync.dma_start(lists["n3"][:], n3)
+        gain = sb("gain", [P, PACK], F32)
+        nc.gpsimd.dma_start(gain[:], gn.rearrange("(p t) o -> p (t o)", t=PACK))
+
+        identity = sb("identity", [P, P], F32)
+        make_identity(nc, identity[:])
+
+        d_scale_picked = sb("d_scale_picked", [P, S], U8)
+        nc.vector.tensor_copy(d_scale_picked[:], d_scale_table[:].indirect(lists["kidx"][:]))
+        key_scales = sb("key_scales", [P, S], U8)
+        nc.vector.tensor_copy(
+            key_scales[:].rearrange("p (t m) -> p m t", t=PACK), d_scale_picked[:].rearrange("p (m t) -> p m t", t=PACK)
+        )
+        for j in range(2):
+            nc.scalar.dma_start(key_scales[2 + j : P : 32, :].bitcast(I32), key_scales[16 + j : P : 32, :].bitcast(I32))
+        d_word_picked = sb("d_word_picked", [P, S], U32)
+        nc.vector.tensor_copy(d_word_picked[:], d_word_table[:].indirect(lists["kidx"][:]))
+        key_words = sb("key_words", [P, S], U32)
+        nc.vector.tensor_copy(
+            key_words[:].bitcast(I32).rearrange("p (t m) -> p m t", t=PACK),
+            d_word_picked[:].bitcast(I32).rearrange("p (m t) -> p m t", t=PACK),
+        )
+        w_raw = sb("w_raw", [P, PACK, S], F32, tag="d_word_table")
+        nc.sync.dma_start(w_raw[:], w1.rearrange("(p j) n -> p j n", j=PACK))
+        query_scales = sb("query_scales", [P, S], U8)
+        nc.vector.tensor_copy(query_scales[:], x_scale_table[:].indirect(lists["offs"][:]))
+        query_words = sb("query_words", [P, S], U32)
+        nc.vector.tensor_copy(query_words[:], x_word_table[:].indirect(lists["offs"][:]))
+
+        gain_pair = sb("gain_pair", [P, PACK], F32)
+        gain_self = sb("gain_self", [P, PACK], F32)
+        nc.vector.tensor_scalar(gain_pair[:], gain[:], -MU, None, ALU.mult)
+        nc.vector.tensor_scalar(gain_self[:], gain[:], -(1.0 - MU) * 0.6, None, ALU.mult)
+
+        window = []
+        for t in range(PACK):
+            scores = psum.tile([P, S], F32, name="scores", tag="row%d" % t)
+            cols = slice(t * P, (t + 1) * P)
+            nc.tensor.matmul_mx(
+                out=scores[:],
+                lhsT=key_words[:, cols].bitcast(FP8X4),
+                lhsT_scale=key_scales[:, cols],
+                rhs=query_words[:].bitcast(FP8X4),
+                rhs_scale=query_scales[:],
+                start=True,
+                stop=True,
+            )
+            window.append(sb("window%d" % t, [P, S], F32))
+            nc.scalar.activation(window[t][:], scores[:], ACT.Copy, scale=-0.0625 * 5.0 / 3.0)
+
+        w_grouped = sb("w_grouped", [P, PACK * S], BF16)
+        w_words = sb("w_words", [P, S], U32)
+        w_scales = sb("w_scales", [P, S], U8)
+
+        pair_sum, inv_root, self_term, diff_sq, rest_sq = [], [], [], [], []
+
+        def add_turned(bank, first, second):
+            for t in range(PACK):
+                nc.tensor.matmul(bank[:, t, :], first(t), identity[:], start=(t == 0), stop=False, is_transpose=True)
+            for t in range(PACK):
+                nc.tensor.matmul(bank[:, t, :], second(t), identity[:], start=False, stop=(t == PACK - 1), is_transpose=True)
+
+        def gather_chunk(c):
+            list_cols = slice(c * LIST_COLS, (c + 1) * LIST_COLS)
+            cols = slice(c * CHUNK, (c + 1) * CHUNK)
+            pa = sb("pa%d" % c, [P, PACK, CHUNK], F32)
+            pb_neg = sb("pb_neg%d" % c, [P, PACK, CHUNK], F32)
+            for t in range(PACK):
+                nc.vector.tensor_scalar(
+                    pa[:, t, :], window[t][:].indirect(lists["n1"][:, list_cols]), -0.6, 0.0, ALU.mult, ALU.add
+                )
+            for t in range(PACK):
+                nc.vector.tensor_scalar(
+                    pb_neg[:, t, :], window[t][:].indirect(lists["n2"][:, list_cols]), 0.6, 0.0, ALU.mult, ALU.add
+                )
+            pair_sum.append(sb("pair_sum%d" % c, [P, PACK, CHUNK], F32))
+            nc.vector.tensor_tensor(pair_sum[c][:], pa[:], pb_neg[:], ALU.subtract)
+
+            diff_t = psum.tile([P, PACK, CHUNK], F32, name="diff_t", tag="diff_t")
+            add_turned(diff_t, lambda t: pa[:, t, :], lambda t: pb_neg[:, t, :])
+            diff_sq.append(sb("diff_sq%d" % c, [P, PACK, CHUNK], F32))
+            nc.scalar.activation(diff_sq[c][:], diff_t[:], ACT.Square, scale=0.5**0.5)
+            if c > 0:
+                root_chunk(c - 1)
+            rest_t = psum.tile([P, PACK, CHUNK], F32, name="rest_t", tag="rest_t")
+            add_turned(rest_t, lambda t: window[t][:, cols], lambda t: pair_sum[c][:, t, :])
+            rest_sq.append(sb("rest_sq%d" % c, [P, PACK, CHUNK], F32))
+            nc.scalar.activation(rest_sq[c][:], rest_t[:], ACT.Square, scale=(1.0 - 2.0 * MU) * 0.5**0.5)
+
+        def root_chunk(c):
+            spread = psum.tile([P, PACK, CHUNK], F32, name="spread", tag="spread%d" % (c % 2))
+            add_turned(spread, lambda t: diff_sq[c][:, t, :], lambda t: rest_sq[c][:, t, :])
+            inv_root.append(sb("inv_root%d" % c, [P, PACK, CHUNK], F32))
+            nc.scalar.activation(inv_root[c][:], spread[:], ACT.Abs_reciprocal_sqrt, bias=0.25)
+
+        def weights_piece(i):
+            m = slice(i * 32, (i + 1) * 32)
+            nc.scalar.copy(
+                w_grouped[:].rearrange("p (t m j) -> p m j t", t=PACK, j=PACK)[:, m],
+                w_raw[:].rearrange("p j (m t) -> p m j t", t=PACK)[:, m],
+            )
+
+        hidden = [psum.tile([P, S], F32, name="hidden", tag="row%d" % t) for t in range(PACK)]
+        h_rows = [sb("h_rows%d" % t, [P, S], F32) for t in range(PACK)]
+
+        def finish_chunk(c):
+            cols = slice(c * CHUNK, (c + 1) * CHUNK)
+            top = sb("top%d" % c, [P, PACK, CHUNK], F32)
+            for t in range(PACK):
+                nc.vector.scalar_tensor_tensor(
+                    top[:, t, :], pair_sum[c][:, t, :], gain_pair[:, t : t + 1], self_term[t][:, cols], ALU.mult, ALU.add
+                )
+            z = sb("z%d" % c, [P, CHUNK * PACK], BF16)
+            nc.vector.tensor_tensor(
+                z[:].rearrange("p (g i t) -> p g t i", i=4, t=PACK),
+                top[:].rearrange("p t (g i) -> p g t i", i=4),
+                inv_root[c][:].rearrange("p t (g i) -> p g t i", i=4),
+                ALU.mult,
+            )
+            z_words = sb("z_words%d" % c, [P, CHUNK], U32)
+            z_scales = sb("z_scales%d" % c, [P, CHUNK], U8)
+            nc.vector.quantize_mx(out=z_words[:].bitcast(FP8X4), scales=z_scales[:], in_=z[:])
+            for t in range(PACK):
+                rows = slice(t * P, (t + 1) * P)
+                nc.tensor.matmul_mx(
+                    out=hidden[t][:, cols],
+                    lhsT=w_words[:, rows].bitcast(FP8X4),
+                    lhsT_scale=w_scales[:, rows],
+                    rhs=z_words[:].bitcast(FP8X4),
+                    rhs_scale=z_scales[:],
+                    start=True,
+                    stop=True,
+                )
+
+        for c in range(CHUNKS):
+            gather_chunk(c)
+        root_chunk(CHUNKS - 1)
+        for t in range(PACK):
+            self_term.append(sb("self_term%d" % t, [P, S], F32))
+            nc.scalar.activation(self_term[t][:], window[t][:], ACT.Copy, scale=gain_self[:, t : t + 1])
+        for i in range(4):
+            weights_piece(i)
+        nc.vector.quantize_mx(out=w_words[:].bitcast(FP8X4), scales=w_scales[:], in_=w_grouped[:])
+        finish_chunk(0)
+        finish_chunk(1)
+        for t in range(PACK):
+            nc.scalar.copy(h_rows[t][:, 0:HALF], hidden[t][:, 0:HALF])
+        finish_chunk(2)
+        finish_chunk(3)
+        for t in range(PACK):
+            nc.vector.tensor_copy(h_rows[t][:, HALF:S], hidden[t][:, HALF:S])
+
+        out_rows = out.rearrange("(p t) n -> p t n", t=PACK)
+        for t in range(PACK):
+            gate = sb("gate%d" % t, [P, S], F32)
+            result = sb("result%d" % t, [P, S], F32)
+            for half in range(2):
+                cols = slice(half * HALF, (half + 1) * HALF)
+                list_cols = slice(half * HALF // 16, (half + 1) * HALF // 16)
+                nc.scalar.activation(gate[:, cols], h_rows[t][:].indirect(lists["n3"][:, list_cols]), ACT.Sigmoid)
+                nc.vector.tensor_tensor(result[:, cols], hidden[t][:, cols], gate[:, cols], ALU.mult)
+                nc.sync.dma_start(out_rows[:, t, cols], result[:, cols])

@@ -45,34 +45,29 @@ def tile_picked_keystdgate_none_p_kernel(
         d_scale_table = sb("d_scale_table", [P, TABLE], U8)
         x_scale_table = sb("x_scale_table", [P, TABLE], U8)
         d_word_table = sb("d_word_table", [P, TABLE], U32)
-        x_word_table = sb("x_word_table", [P, TABLE], U32)
         nc.vector.memset(d_scale_table[:].bitcast(I32), 0)
         nc.gpsimd.memset(x_scale_table[:].bitcast(I32), 0)
 
-        warm = sb("warm", [P, 2], F32)
-        nc.vector.memset(warm[:, 0:1], 1.0)
-        nc.scalar.activation(warm[:, 1:2], warm[:, 0:1], ACT.Abs_reciprocal_sqrt)
-
-        nc.sync.dma_start(lists["kidx"][:], kidx)
+        nc.scalar.dma_start(d_word_table[:].bitcast(I32), d_words[0].rearrange("p n t -> p (n t)").bitcast(I32))
+        for name, source in (("kidx", kidx), ("offs", offs), ("n1", n1), ("n2", n2), ("n3", n3)):
+            nc.sync.dma_start(lists[name][:], source)
         for j in range(2):
-            nc.scalar.dma_start(d_scale_table[j:P:16, :].bitcast(I32), d_scales[0][j:16:2, :].bitcast(I32))
-        nc.sync.dma_start(d_word_table[:].bitcast(I32), d_words[0].rearrange("p n t -> p (n t)").bitcast(I32))
-        nc.sync.dma_start(lists["offs"][:], offs)
-        nc.sync.dma_start(x_word_table[:].bitcast(I32), x_words[0].rearrange("p n t -> p (n t)").bitcast(I32))
+            nc.sync.dma_start(d_scale_table[j:P:16, :].bitcast(I32), d_scales[0][j:16:2, :].bitcast(I32))
         for q in range(4):
-            nc.gpsimd.dma_start(
+            nc.sync.dma_start(
                 x_scale_table[32 * q : 32 * q + 4, :].bitcast(I32), x_scales[0][4 * q : 4 * q + 4, :].bitcast(I32)
             )
-        nc.sync.dma_start(lists["n1"][:], n1)
-        nc.sync.dma_start(lists["n2"][:], n2)
-        nc.sync.dma_start(lists["n3"][:], n3)
-        gain = sb("gain", [P, PACK], F32)
-        nc.gpsimd.dma_start(gain[:], gn.rearrange("(p t) o -> p (t o)", t=PACK))
+
+        warm = sb("warm", [P, 2], F32, tag="x_word_table")
+        nc.vector.memset(warm[:, 0:1], 1.0)
+        nc.scalar.activation(warm[:, 1:2], warm[:, 0:1], ACT.Abs_reciprocal_sqrt)
+        x_word_table = sb("x_word_table", [P, TABLE], U32)
+        nc.scalar.dma_start(x_word_table[:].bitcast(I32), x_words[0].rearrange("p n t -> p (n t)").bitcast(I32))
 
         identity = sb("identity", [P, P], F32)
         make_identity(nc, identity[:])
 
-        d_scale_picked = sb("d_scale_picked", [P, S], U8)
+        d_scale_picked = sb("d_scale_picked", [P, S], U8, tag="d_picked")
         nc.vector.tensor_copy(d_scale_picked[:], d_scale_table[:].indirect(lists["kidx"][:]))
         key_scales = sb("key_scales", [P, S], U8)
         nc.vector.tensor_copy(
@@ -80,7 +75,9 @@ def tile_picked_keystdgate_none_p_kernel(
         )
         for j in range(2):
             nc.scalar.dma_start(key_scales[2 + j : P : 32, :].bitcast(I32), key_scales[16 + j : P : 32, :].bitcast(I32))
-        d_word_picked = sb("d_word_picked", [P, S], U32)
+        gain = sb("gain", [P, PACK], F32, tag="d_scale_table")
+        nc.sync.dma_start(gain[:], gn.rearrange("(p t) o -> p (t o)", t=PACK))
+        d_word_picked = sb("d_word_picked", [P, S], U32, tag="d_picked")
         nc.vector.tensor_copy(d_word_picked[:], d_word_table[:].indirect(lists["kidx"][:]))
         key_words = sb("key_words", [P, S], U32)
         nc.vector.tensor_copy(
@@ -91,8 +88,12 @@ def tile_picked_keystdgate_none_p_kernel(
         nc.sync.dma_start(w_raw[:], w1.rearrange("(p j) n -> p j n", j=PACK))
         query_scales = sb("query_scales", [P, S], U8)
         nc.vector.tensor_copy(query_scales[:], x_scale_table[:].indirect(lists["offs"][:]))
-        query_words = sb("query_words", [P, S], U32)
-        nc.vector.tensor_copy(query_words[:], x_word_table[:].indirect(lists["offs"][:]))
+        query_words = sb("query_words", [P, S], U32, tag="x_scale_table")
+        for h in range(2):
+            nc.vector.tensor_copy(
+                query_words[:, h * HALF : (h + 1) * HALF],
+                x_word_table[:].indirect(lists["offs"][:, h * HALF // 16 : (h + 1) * HALF // 16]),
+            )
 
         gain_pair = sb("gain_pair", [P, PACK], F32)
         gain_self = sb("gain_self", [P, PACK], F32)
@@ -102,63 +103,82 @@ def tile_picked_keystdgate_none_p_kernel(
         window = []
         for t in range(PACK):
             scores = psum.tile([P, S], F32, name="scores", tag="row%d" % t)
-            cols = slice(t * P, (t + 1) * P)
-            nc.tensor.matmul_mx(
-                out=scores[:],
-                lhsT=key_words[:, cols].bitcast(FP8X4),
-                lhsT_scale=key_scales[:, cols],
-                rhs=query_words[:].bitcast(FP8X4),
-                rhs_scale=query_scales[:],
-                start=True,
-                stop=True,
-            )
+            keys = slice(t * P, (t + 1) * P)
             window.append(sb("window%d" % t, [P, S], F32))
-            nc.scalar.activation(window[t][:], scores[:], ACT.Copy, scale=-0.0625 * 5.0 / 3.0)
+            for cols in (slice(0, HALF), slice(HALF, S)) if t == 0 else (slice(0, S),):
+                nc.tensor.matmul_mx(
+                    out=scores[:, cols],
+                    lhsT=key_words[:, keys].bitcast(FP8X4),
+                    lhsT_scale=key_scales[:, keys],
+                    rhs=query_words[:, cols].bitcast(FP8X4),
+                    rhs_scale=query_scales[:, cols],
+                    start=True,
+                    stop=True,
+                )
+                nc.scalar.activation(window[t][:, cols], scores[:, cols], ACT.Copy, scale=-0.0625 * 5.0 / 3.0)
 
         w_grouped = sb("w_grouped", [P, PACK * S], BF16)
         w_words = sb("w_words", [P, S], U32)
         w_scales = sb("w_scales", [P, S], U8)
 
-        pair_sum, inv_root, self_term, diff_sq, rest_sq = [], [], [], [], []
+        def halves(name):
+            return [sb("%s%d" % (name, h), [P, PACK, HALF], F32) for h in range(2)]
 
-        def add_turned(bank, first, second):
-            for t in range(PACK):
-                nc.tensor.matmul(bank[:, t, :], first(t), identity[:], start=(t == 0), stop=False, is_transpose=True)
-            for t in range(PACK):
-                nc.tensor.matmul(bank[:, t, :], second(t), identity[:], start=False, stop=(t == PACK - 1), is_transpose=True)
+        pa, pb_neg, pair_sum, inv_root, top = (halves(n) for n in ("pa", "pb_neg", "pair_sum", "inv_root", "top"))
+        self_term, diff_sq, rest_sq = [], [], []
 
-        def gather_chunk(c):
-            list_cols = slice(c * LIST_COLS, (c + 1) * LIST_COLS)
-            cols = slice(c * CHUNK, (c + 1) * CHUNK)
-            pa = sb("pa%d" % c, [P, PACK, CHUNK], F32)
-            pb_neg = sb("pb_neg%d" % c, [P, PACK, CHUNK], F32)
-            for t in range(PACK):
+        def turn(bank, b, source, start=False, stop=False):
+            nc.tensor.matmul(bank[:, b, :], source, identity[:], start=start, stop=stop, is_transpose=True)
+
+        spread = []
+
+        def gather_unit(u):
+            h, t0 = u // 2, 2 * (u % 2)
+            list_cols = slice(h * HALF // 16, (h + 1) * HALF // 16)
+
+            def block(tile, b, base=0):
+                return tile[:, base + (b % 2) * P : base + (b % 2 + 1) * P]
+
+            rest_t = psum.tile([P, 4, P], F32, name="rest_t", tag="rest_t%d" % (u % 2))
+            for b in range(4):
+                turn(rest_t, b, block(window[t0 + b // 2], b, h * HALF), start=(b == 0))
+            if u > 0:
+                root_unit(u - 1)
+            diff_t = psum.tile([P, 4, P], F32, name="diff_t", tag="diff_t%d" % (u % 2))
+            for t in (t0, t0 + 1):
                 nc.vector.tensor_scalar(
-                    pa[:, t, :], window[t][:].indirect(lists["n1"][:, list_cols]), -0.6, 0.0, ALU.mult, ALU.add
+                    pa[h][:, t, :], window[t][:].indirect(lists["n1"][:, list_cols]), -0.6, 0.0, ALU.mult, ALU.add
                 )
-            for t in range(PACK):
                 nc.vector.tensor_scalar(
-                    pb_neg[:, t, :], window[t][:].indirect(lists["n2"][:, list_cols]), 0.6, 0.0, ALU.mult, ALU.add
+                    pb_neg[h][:, t, :], window[t][:].indirect(lists["n2"][:, list_cols]), 0.6, 0.0, ALU.mult, ALU.add
                 )
-            pair_sum.append(sb("pair_sum%d" % c, [P, PACK, CHUNK], F32))
-            nc.vector.tensor_tensor(pair_sum[c][:], pa[:], pb_neg[:], ALU.subtract)
+                blocks = (2 * (t - t0), 2 * (t - t0) + 1)
+                for b in blocks:
+                    turn(diff_t, b, block(pa[h][:, t, :], b), start=(b == 0))
+                for b in blocks:
+                    turn(diff_t, b, block(pb_neg[h][:, t, :], b), stop=(b == 3))
+            pair = slice(t0, t0 + 2)
+            nc.vector.tensor_tensor(pair_sum[h][:, pair, :], pa[h][:, pair, :], pb_neg[h][:, pair, :], ALU.subtract)
+            diff_sq.append(sb("diff_sq%d" % u, [P, 4, P], F32, tag="d_word_table" if u == 2 else None))
+            nc.scalar.activation(diff_sq[u][:], diff_t[:], ACT.Square, scale=0.5**0.5)
+            for b in range(4):
+                turn(rest_t, b, block(pair_sum[h][:, t0 + b // 2, :], b), stop=(b == 3))
+            rest_sq.append(sb("rest_sq%d" % u, [P, 4, P], F32))
+            nc.scalar.activation(rest_sq[u][:], rest_t[:], ACT.Square, scale=(1.0 - 2.0 * MU) * 0.5**0.5)
+            spread.append(psum.tile([P, 4, P], F32, name="spread", tag="diff_t%d" % (u % 2)))
+            for b in range(4):
+                turn(spread[u], b, diff_sq[u][:, b, :], start=(b == 0))
 
-            diff_t = psum.tile([P, PACK, CHUNK], F32, name="diff_t", tag="diff_t")
-            add_turned(diff_t, lambda t: pa[:, t, :], lambda t: pb_neg[:, t, :])
-            diff_sq.append(sb("diff_sq%d" % c, [P, PACK, CHUNK], F32))
-            nc.scalar.activation(diff_sq[c][:], diff_t[:], ACT.Square, scale=0.5**0.5)
-            if c > 0:
-                root_chunk(c - 1)
-            rest_t = psum.tile([P, PACK, CHUNK], F32, name="rest_t", tag="rest_t")
-            add_turned(rest_t, lambda t: window[t][:, cols], lambda t: pair_sum[c][:, t, :])
-            rest_sq.append(sb("rest_sq%d" % c, [P, PACK, CHUNK], F32))
-            nc.scalar.activation(rest_sq[c][:], rest_t[:], ACT.Square, scale=(1.0 - 2.0 * MU) * 0.5**0.5)
-
-        def root_chunk(c):
-            spread = psum.tile([P, PACK, CHUNK], F32, name="spread", tag="spread%d" % (c % 2))
-            add_turned(spread, lambda t: diff_sq[c][:, t, :], lambda t: rest_sq[c][:, t, :])
-            inv_root.append(sb("inv_root%d" % c, [P, PACK, CHUNK], F32))
-            nc.scalar.activation(inv_root[c][:], spread[:], ACT.Abs_reciprocal_sqrt, bias=0.25)
+        def root_unit(u):
+            h, t0 = u // 2, 2 * (u % 2)
+            for b in range(4):
+                turn(spread[u], b, rest_sq[u][:, b, :], stop=(b == 3))
+            nc.scalar.activation(
+                inv_root[h][:, t0 : t0 + 2, :].rearrange("p t n -> p (t n)"),
+                spread[u][:].rearrange("p b n -> p (b n)"),
+                ACT.Abs_reciprocal_sqrt,
+                bias=0.25,
+            )
 
         def weights_piece(i):
             m = slice(i * 32, (i + 1) * 32)
@@ -170,27 +190,35 @@ def tile_picked_keystdgate_none_p_kernel(
         hidden = [psum.tile([P, S], F32, name="hidden", tag="row%d" % t) for t in range(PACK)]
         h_rows = [sb("h_rows%d" % t, [P, S], F32) for t in range(PACK)]
 
-        def finish_chunk(c):
-            cols = slice(c * CHUNK, (c + 1) * CHUNK)
-            top = sb("top%d" % c, [P, PACK, CHUNK], F32)
+        def top_half(h):
             for t in range(PACK):
                 nc.vector.scalar_tensor_tensor(
-                    top[:, t, :], pair_sum[c][:, t, :], gain_pair[:, t : t + 1], self_term[t][:, cols], ALU.mult, ALU.add
+                    top[h][:, t, :],
+                    pair_sum[h][:, t, :],
+                    gain_pair[:, t : t + 1],
+                    self_term[t][:, h * HALF : (h + 1) * HALF],
+                    ALU.mult,
+                    ALU.add,
                 )
-            z = sb("z%d" % c, [P, CHUNK * PACK], BF16)
+
+        def divide(h, lo, width):
+            z = sb("z%d_%d" % (h, lo), [P, width * PACK], BF16)
             nc.vector.tensor_tensor(
                 z[:].rearrange("p (g i t) -> p g t i", i=4, t=PACK),
-                top[:].rearrange("p t (g i) -> p g t i", i=4),
-                inv_root[c][:].rearrange("p t (g i) -> p g t i", i=4),
+                top[h][:, :, lo : lo + width].rearrange("p t (g i) -> p g t i", i=4),
+                inv_root[h][:, :, lo : lo + width].rearrange("p t (g i) -> p g t i", i=4),
                 ALU.mult,
             )
-            z_words = sb("z_words%d" % c, [P, CHUNK], U32)
-            z_scales = sb("z_scales%d" % c, [P, CHUNK], U8)
+            return z
+
+        def second_product(z, h, lo, width):
+            z_words = sb("z_words%d_%d" % (h, lo), [P, width], U32, tag="rest_sq3" if h == 0 else None)
+            z_scales = sb("z_scales%d_%d" % (h, lo), [P, width], U8)
             nc.vector.quantize_mx(out=z_words[:].bitcast(FP8X4), scales=z_scales[:], in_=z[:])
             for t in range(PACK):
                 rows = slice(t * P, (t + 1) * P)
                 nc.tensor.matmul_mx(
-                    out=hidden[t][:, cols],
+                    out=hidden[t][:, h * HALF + lo : h * HALF + lo + width],
                     lhsT=w_words[:, rows].bitcast(FP8X4),
                     lhsT_scale=w_scales[:, rows],
                     rhs=z_words[:].bitcast(FP8X4),
@@ -199,21 +227,29 @@ def tile_picked_keystdgate_none_p_kernel(
                     stop=True,
                 )
 
-        for c in range(CHUNKS):
-            gather_chunk(c)
-        root_chunk(CHUNKS - 1)
+        gather_unit(0)
         for t in range(PACK):
             self_term.append(sb("self_term%d" % t, [P, S], F32))
             nc.scalar.activation(self_term[t][:], window[t][:], ACT.Copy, scale=gain_self[:, t : t + 1])
+        gather_unit(1)
         for i in range(4):
             weights_piece(i)
+        gather_unit(2)
+        gather_unit(3)
+        root_unit(3)
+        warm_gate = sb("warm_gate", [P, 1], F32)
+        nc.scalar.activation(warm_gate[:], inv_root[1][:, PACK - 1, 0:1], ACT.Sigmoid)
+        top_half(0)
         nc.vector.quantize_mx(out=w_words[:].bitcast(FP8X4), scales=w_scales[:], in_=w_grouped[:])
-        finish_chunk(0)
-        finish_chunk(1)
+        z_first = divide(0, 0, HALF)
+        top_half(1)
+        second_product(z_first, 0, 0, HALF)
         for t in range(PACK):
             nc.scalar.copy(h_rows[t][:, 0:HALF], hidden[t][:, 0:HALF])
-        finish_chunk(2)
-        finish_chunk(3)
+        z_third = divide(1, 0, CHUNK)
+        z_last = divide(1, CHUNK, CHUNK)
+        second_product(z_third, 1, 0, CHUNK)
+        second_product(z_last, 1, CHUNK, CHUNK)
         for t in range(PACK):
             nc.vector.tensor_copy(h_rows[t][:, HALF:S], hidden[t][:, HALF:S])
 

@@ -17,14 +17,16 @@ P = 128
 PACK = 4
 TABLE = 2048
 S = 512
-CHUNK = 128
-CHUNKS = S // CHUNK
-LIST_COLS = CHUNK // 16
 HALF = S // 2
+QUARTER = S // 4
+LIST = 16
 
 FLOPS = 2 * 2 * 512 * 512 * 512
 
 MU = 0.3125
+WINDOW = -5.0 / 3.0
+DIFF_SCALE = 0.5**0.5 / WINDOW
+REST_SCALE = (1.0 - 2.0 * MU) * 0.5**0.5 / WINDOW
 
 
 def tile_picked_keystdgate_none_p_kernel(
@@ -40,15 +42,16 @@ def tile_picked_keystdgate_none_p_kernel(
 
         lists = {}
         for name in ("kidx", "offs", "n1", "n2", "n3"):
-            lists[name] = keep.tile([P, S // 16], U16, name="list_" + name)
+            lists[name] = keep.tile([P, S // LIST], U16, name="list_" + name)
+
+        def entries(name, lo, hi):
+            return lists[name][:, lo // LIST : hi // LIST]
 
         d_scale_table = sb("d_scale_table", [P, TABLE], U8)
         x_scale_table = sb("x_scale_table", [P, TABLE], U8)
-        d_word_table = sb("d_word_table", [P, TABLE], U32)
         nc.vector.memset(d_scale_table[:].bitcast(I32), 0)
         nc.gpsimd.memset(x_scale_table[:].bitcast(I32), 0)
 
-        nc.scalar.dma_start(d_word_table[:].bitcast(I32), d_words[0].rearrange("p n t -> p (n t)").bitcast(I32))
         for name, source in (("kidx", kidx), ("offs", offs), ("n1", n1), ("n2", n2), ("n3", n3)):
             nc.sync.dma_start(lists[name][:], source)
         for j in range(2):
@@ -58,10 +61,13 @@ def tile_picked_keystdgate_none_p_kernel(
                 x_scale_table[32 * q : 32 * q + 4, :].bitcast(I32), x_scales[0][4 * q : 4 * q + 4, :].bitcast(I32)
             )
 
-        warm = sb("warm", [P, 2], F32, tag="x_word_table")
-        nc.vector.memset(warm[:, 0:1], 1.0)
-        nc.scalar.activation(warm[:, 1:2], warm[:, 0:1], ACT.Abs_reciprocal_sqrt)
+        warm_in = sb("warm_in", [P, 1], F32, tag="d_word_table")
+        warm_out = sb("warm_out", [P, 1], F32, tag="x_word_table")
+        nc.vector.memset(warm_in[:], 1.0)
+        nc.scalar.activation(warm_out[:], warm_in[:], ACT.Abs_reciprocal_sqrt)
+        d_word_table = sb("d_word_table", [P, TABLE], U32)
         x_word_table = sb("x_word_table", [P, TABLE], U32)
+        nc.scalar.dma_start(d_word_table[:].bitcast(I32), d_words[0].rearrange("p n t -> p (n t)").bitcast(I32))
         nc.scalar.dma_start(x_word_table[:].bitcast(I32), x_words[0].rearrange("p n t -> p (n t)").bitcast(I32))
 
         identity = sb("identity", [P, P], F32)
@@ -74,9 +80,11 @@ def tile_picked_keystdgate_none_p_kernel(
             key_scales[:].rearrange("p (t m) -> p m t", t=PACK), d_scale_picked[:].rearrange("p (m t) -> p m t", t=PACK)
         )
         for j in range(2):
-            nc.scalar.dma_start(key_scales[2 + j : P : 32, :].bitcast(I32), key_scales[16 + j : P : 32, :].bitcast(I32))
+            nc.sync.dma_start(key_scales[2 + j : P : 32, :].bitcast(I32), key_scales[16 + j : P : 32, :].bitcast(I32))
         gain = sb("gain", [P, PACK], F32, tag="d_scale_table")
         nc.sync.dma_start(gain[:], gn.rearrange("(p t) o -> p (t o)", t=PACK))
+        query_scales = sb("query_scales", [P, S], U8)
+        nc.vector.tensor_copy(query_scales[:], x_scale_table[:].indirect(lists["offs"][:]))
         d_word_picked = sb("d_word_picked", [P, S], U32, tag="d_picked")
         nc.vector.tensor_copy(d_word_picked[:], d_word_table[:].indirect(lists["kidx"][:]))
         key_words = sb("key_words", [P, S], U32)
@@ -86,19 +94,14 @@ def tile_picked_keystdgate_none_p_kernel(
         )
         w_raw = sb("w_raw", [P, PACK, S], F32, tag="d_word_table")
         nc.sync.dma_start(w_raw[:], w1.rearrange("(p j) n -> p j n", j=PACK))
-        query_scales = sb("query_scales", [P, S], U8)
-        nc.vector.tensor_copy(query_scales[:], x_scale_table[:].indirect(lists["offs"][:]))
         query_words = sb("query_words", [P, S], U32, tag="x_scale_table")
-        for h in range(2):
-            nc.vector.tensor_copy(
-                query_words[:, h * HALF : (h + 1) * HALF],
-                x_word_table[:].indirect(lists["offs"][:, h * HALF // 16 : (h + 1) * HALF // 16]),
-            )
+        for lo in (0, HALF):
+            nc.vector.tensor_copy(query_words[:, lo : lo + HALF], x_word_table[:].indirect(entries("offs", lo, lo + HALF)))
 
-        gain_pair = sb("gain_pair", [P, PACK], F32)
         gain_self = sb("gain_self", [P, PACK], F32)
-        nc.vector.tensor_scalar(gain_pair[:], gain[:], -MU, None, ALU.mult)
-        nc.vector.tensor_scalar(gain_self[:], gain[:], -(1.0 - MU) * 0.6, None, ALU.mult)
+        gain_pair = sb("gain_pair", [P, PACK], F32)
+        nc.vector.tensor_scalar(gain_pair[:], gain[:], -MU / WINDOW, None, ALU.mult)
+        nc.vector.tensor_scalar(gain_self[:], gain[:], (1.0 - MU) / WINDOW, None, ALU.mult)
 
         window = []
         for t in range(PACK):
@@ -115,79 +118,98 @@ def tile_picked_keystdgate_none_p_kernel(
                     start=True,
                     stop=True,
                 )
-                nc.scalar.activation(window[t][:, cols], scores[:, cols], ACT.Copy, scale=-0.0625 * 5.0 / 3.0)
+                nc.scalar.activation(window[t][:, cols], scores[:, cols], ACT.Copy, scale=0.0625 * WINDOW)
 
-        w_grouped = sb("w_grouped", [P, PACK * S], BF16)
+        shifted = sb("shifted", [P, 2, S], F32)
+        for t in range(2):
+            nc.scalar.activation(shifted[:, t, :], window[t][:], ACT.Copy, scale=WINDOW)
+
         w_words = sb("w_words", [P, S], U32)
         w_scales = sb("w_scales", [P, S], U8)
 
         def halves(name):
             return [sb("%s%d" % (name, h), [P, PACK, HALF], F32) for h in range(2)]
 
-        pa, pb_neg, pair_sum, inv_root, top = (halves(n) for n in ("pa", "pb_neg", "pair_sum", "inv_root", "top"))
-        self_term, diff_sq, rest_sq = [], [], []
+        pair_sum, inv_root, top = (halves(name) for name in ("pair_sum", "inv_root", "top"))
+        self_term, w_grouped, diff_sq, rest_sq, spread, hidden = [], [], [], [], [], []
 
         def turn(bank, b, source, start=False, stop=False):
             nc.tensor.matmul(bank[:, b, :], source, identity[:], start=start, stop=stop, is_transpose=True)
 
-        spread = []
+        def block(rows, b):
+            return rows[:, b // 2, (b % 2) * P : (b % 2 + 1) * P]
 
-        def gather_unit(u):
-            h, t0 = u // 2, 2 * (u % 2)
-            list_cols = slice(h * HALF // 16, (h + 1) * HALF // 16)
-
-            def block(tile, b, base=0):
-                return tile[:, base + (b % 2) * P : base + (b % 2 + 1) * P]
-
-            rest_t = psum.tile([P, 4, P], F32, name="rest_t", tag="rest_t%d" % (u % 2))
-            for b in range(4):
-                turn(rest_t, b, block(window[t0 + b // 2], b, h * HALF), start=(b == 0))
-            if u > 0:
-                root_unit(u - 1)
-            diff_t = psum.tile([P, 4, P], F32, name="diff_t", tag="diff_t%d" % (u % 2))
-            for t in (t0, t0 + 1):
+        def gather(u):
+            h, t0 = u % 2, 2 * (u // 2)
+            lo, hi = h * HALF, (h + 1) * HALF
+            pa_neg = sb("pa_neg%d" % u, [P, 2, HALF], F32)
+            both = pair_sum[h][:, t0 : t0 + 2, :]
+            for i in range(2):
                 nc.vector.tensor_scalar(
-                    pa[h][:, t, :], window[t][:].indirect(lists["n1"][:, list_cols]), -0.6, 0.0, ALU.mult, ALU.add
+                    pa_neg[:, i, :], window[t0 + i][:].indirect(entries("n1", lo, hi)), -1.0, 0.0, ALU.mult, ALU.add
                 )
-                nc.vector.tensor_scalar(
-                    pb_neg[h][:, t, :], window[t][:].indirect(lists["n2"][:, list_cols]), 0.6, 0.0, ALU.mult, ALU.add
+            for i in range(2):
+                nc.vector.tensor_tensor(
+                    both[:, i, :], window[t0 + i][:].indirect(entries("n2", lo, hi)), pa_neg[:, i, :], ALU.subtract
                 )
-                blocks = (2 * (t - t0), 2 * (t - t0) + 1)
-                for b in blocks:
-                    turn(diff_t, b, block(pa[h][:, t, :], b), start=(b == 0))
-                for b in blocks:
-                    turn(diff_t, b, block(pb_neg[h][:, t, :], b), stop=(b == 3))
-            pair = slice(t0, t0 + 2)
-            nc.vector.tensor_tensor(pair_sum[h][:, pair, :], pa[h][:, pair, :], pb_neg[h][:, pair, :], ALU.subtract)
-            diff_sq.append(sb("diff_sq%d" % u, [P, 4, P], F32, tag="d_word_table" if u == 2 else None))
-            nc.scalar.activation(diff_sq[u][:], diff_t[:], ACT.Square, scale=0.5**0.5)
+            return pa_neg, both
+
+        def turned_squares(u, pa_neg, both):
+            diff_t = psum.tile([P, 4, P], F32, name="diff_t", tag="diff_t%d" % u)
+            for twice in range(2):
+                for b in range(4):
+                    turn(diff_t, b, block(pa_neg, b), start=(twice == 0 and b == 0))
             for b in range(4):
-                turn(rest_t, b, block(pair_sum[h][:, t0 + b // 2, :], b), stop=(b == 3))
+                turn(diff_t, b, block(both, b), stop=(b == 3))
+            diff_sq.append(sb("diff_sq%d" % u, [P, 4, P], F32))
+            nc.scalar.activation(diff_sq[u][:], diff_t[:], ACT.Square, scale=DIFF_SCALE)
+            rest_t = psum.tile([P, 4, P], F32, name="rest_t", tag="rest_t%d" % u)
+            for b in range(4):
+                turn(rest_t, b, block(both, b), start=(b == 0))
+            for b in range(4):
+                turn(rest_t, b, block(shifted[:, :, u * HALF : (u + 1) * HALF], b), stop=(b == 3))
             rest_sq.append(sb("rest_sq%d" % u, [P, 4, P], F32))
-            nc.scalar.activation(rest_sq[u][:], rest_t[:], ACT.Square, scale=(1.0 - 2.0 * MU) * 0.5**0.5)
-            spread.append(psum.tile([P, 4, P], F32, name="spread", tag="diff_t%d" % (u % 2)))
+            nc.scalar.activation(rest_sq[u][:], rest_t[:], ACT.Square, scale=REST_SCALE)
+            spread.append(psum.tile([P, 4, P], F32, name="spread", tag="diff_t%d" % u))
             for b in range(4):
                 turn(spread[u], b, diff_sq[u][:, b, :], start=(b == 0))
 
-        def root_unit(u):
-            h, t0 = u // 2, 2 * (u % 2)
+        def turned_root(u):
             for b in range(4):
                 turn(spread[u], b, rest_sq[u][:, b, :], stop=(b == 3))
             nc.scalar.activation(
-                inv_root[h][:, t0 : t0 + 2, :].rearrange("p t n -> p (t n)"),
+                inv_root[u][:, 0:2, :].rearrange("p t n -> p (t n)"),
                 spread[u][:].rearrange("p b n -> p (b n)"),
                 ACT.Abs_reciprocal_sqrt,
                 bias=0.25,
             )
 
-        def weights_piece(i):
-            m = slice(i * 32, (i + 1) * 32)
+        def plain_squares(u, pa_neg, both, rest_out, diff_out):
+            h = u % 2
+            rest = sb("rest%d" % u, [P, 2, HALF], F32)
+            for i in range(2):
+                nc.vector.scalar_tensor_tensor(
+                    rest[:, i, :], window[2 + i][:, h * HALF : (h + 1) * HALF], WINDOW, both[:, i, :], ALU.mult, ALU.add
+                )
+            rest_sq.append(rest_out)
+            diff_sq.append(diff_out)
+            nc.scalar.activation(rest_out, rest[:], ACT.Square, scale=REST_SCALE)
+            diff = sb("diff%d" % u, [P, 2, HALF], F32)
+            nc.vector.scalar_tensor_tensor(diff[:], pa_neg[:], 2.0, both, ALU.mult, ALU.add)
+            nc.scalar.activation(diff_out, diff[:], ACT.Square, scale=DIFF_SCALE)
+
+        def plain_root(u):
+            squares = sb("squares%d" % u, [P, 2, HALF], F32)
+            nc.vector.tensor_tensor(squares[:], diff_sq[u], rest_sq[u], ALU.add)
+            nc.scalar.activation(inv_root[u % 2][:, 2:4, :], squares[:], ACT.Abs_reciprocal_sqrt, bias=0.25)
+
+        def group_weights(i, tag):
+            w_grouped.append(sb("w_grouped%d" % i, [P, 2 * S], BF16, tag=tag))
             nc.scalar.copy(
-                w_grouped[:].rearrange("p (t m j) -> p m j t", t=PACK, j=PACK)[:, m],
-                w_raw[:].rearrange("p j (m t) -> p m j t", t=PACK)[:, m],
+                w_grouped[i][:].rearrange("p (t m j) -> p m j t", t=2, j=PACK),
+                w_raw[:].rearrange("p j (m t) -> p m j t", t=PACK)[:, :, :, 2 * i : 2 * i + 2],
             )
 
-        hidden = [psum.tile([P, S], F32, name="hidden", tag="row%d" % t) for t in range(PACK)]
         h_rows = [sb("h_rows%d" % t, [P, S], F32) for t in range(PACK)]
 
         def top_half(h):
@@ -211,55 +233,85 @@ def tile_picked_keystdgate_none_p_kernel(
             )
             return z
 
-        def second_product(z, h, lo, width):
-            z_words = sb("z_words%d_%d" % (h, lo), [P, width], U32, tag="rest_sq3" if h == 0 else None)
-            z_scales = sb("z_scales%d_%d" % (h, lo), [P, width], U8)
+        def quantise(z, name, width):
+            z_words = sb("z_words" + name, [P, width], U32)
+            z_scales = sb("z_scales" + name, [P, width], U8)
             nc.vector.quantize_mx(out=z_words[:].bitcast(FP8X4), scales=z_scales[:], in_=z[:])
-            for t in range(PACK):
-                rows = slice(t * P, (t + 1) * P)
-                nc.tensor.matmul_mx(
-                    out=hidden[t][:, h * HALF + lo : h * HALF + lo + width],
-                    lhsT=w_words[:, rows].bitcast(FP8X4),
-                    lhsT_scale=w_scales[:, rows],
-                    rhs=z_words[:].bitcast(FP8X4),
-                    rhs_scale=z_scales[:],
-                    start=True,
-                    stop=True,
-                )
+            return z_words, z_scales
 
-        gather_unit(0)
+        def second_product(t, codes, lo, width):
+            rows = slice(t * P, (t + 1) * P)
+            nc.tensor.matmul_mx(
+                out=hidden[t][:, lo : lo + width],
+                lhsT=w_words[:, rows].bitcast(FP8X4),
+                lhsT_scale=w_scales[:, rows],
+                rhs=codes[0][:].bitcast(FP8X4),
+                rhs_scale=codes[1][:],
+                start=True,
+                stop=True,
+            )
+
+        turned_squares(0, *gather(0))
         for t in range(PACK):
             self_term.append(sb("self_term%d" % t, [P, S], F32))
             nc.scalar.activation(self_term[t][:], window[t][:], ACT.Copy, scale=gain_self[:, t : t + 1])
-        gather_unit(1)
-        for i in range(4):
-            weights_piece(i)
-        gather_unit(2)
-        gather_unit(3)
-        root_unit(3)
+        picked = gather(1)
+        turned_root(0)
+        turned_squares(1, *picked)
+        group_weights(0, "diff_sq0")
+        group_weights(1, "rest_sq0")
+        picked = gather(2)
+        turned_root(1)
+        both_sq = sb("both_sq", [P, 2, 2, HALF], F32, tag="d_word_table")
+        plain_squares(2, *picked, both_sq[:, 0], both_sq[:, 1])
+        picked = gather(3)
+        rest_sq_last = sb("rest_sq3", [P, 2, HALF], F32, tag="rest2")
+        diff_sq_last = sb("diff_sq3", [P, 2, HALF], F32, tag="diff2")
+        plain_squares(3, *picked, rest_sq_last[:], diff_sq_last[:])
+        plain_root(2)
+        for t in range(PACK):
+            hidden.append(psum.tile([P, S], F32, name="hidden", tag="row%d" % t))
+        top_half(0)
+        plain_root(3)
         warm_gate = sb("warm_gate", [P, 1], F32)
         nc.scalar.activation(warm_gate[:], inv_root[1][:, PACK - 1, 0:1], ACT.Sigmoid)
-        top_half(0)
-        nc.vector.quantize_mx(out=w_words[:].bitcast(FP8X4), scales=w_scales[:], in_=w_grouped[:])
+        for i in range(2):
+            cols = slice(i * HALF, (i + 1) * HALF)
+            nc.vector.quantize_mx(out=w_words[:, cols].bitcast(FP8X4), scales=w_scales[:, cols], in_=w_grouped[i][:])
         z_first = divide(0, 0, HALF)
         top_half(1)
-        second_product(z_first, 0, 0, HALF)
+        codes_first = quantise(z_first, "_first", HALF)
+        for t in range(PACK):
+            second_product(t, codes_first, 0, HALF)
+
+        gate_rows = sb("gate_rows", [P, S], F32)
         for t in range(PACK):
             nc.scalar.copy(h_rows[t][:, 0:HALF], hidden[t][:, 0:HALF])
-        z_third = divide(1, 0, CHUNK)
-        z_last = divide(1, CHUNK, CHUNK)
-        second_product(z_third, 1, 0, CHUNK)
-        second_product(z_last, 1, CHUNK, CHUNK)
+        nc.scalar.activation(gate_rows[:, 0:HALF], hidden[0][:, 0:HALF], ACT.Sigmoid)
+        z_third = divide(1, 0, QUARTER)
+        z_last = divide(1, QUARTER, QUARTER)
+        codes_third = quantise(z_third, "_third", QUARTER)
+        codes_last = quantise(z_last, "_last", QUARTER)
         for t in range(PACK):
+            second_product(t, codes_third, HALF, QUARTER)
+            second_product(t, codes_last, HALF + QUARTER, QUARTER)
+        nc.scalar.activation(gate_rows[:, HALF:S], hidden[0][:, HALF:S], ACT.Sigmoid)
+        nc.scalar.copy(h_rows[0][:, HALF:S], hidden[0][:, HALF:S])
+        for t in range(1, PACK):
             nc.vector.tensor_copy(h_rows[t][:, HALF:S], hidden[t][:, HALF:S])
 
         out_rows = out.rearrange("(p t) n -> p t n", t=PACK)
-        for t in range(PACK):
+        result = [sb("result%d" % t, [P, S], F32) for t in range(PACK)]
+        for lo in (0, HALF):
+            cols = slice(lo, lo + HALF)
+            nc.vector.tensor_tensor(
+                result[0][:, cols], gate_rows[:].indirect(entries("n3", lo, lo + HALF)), h_rows[0][:, cols], ALU.mult
+            )
+            nc.sync.dma_start(out_rows[:, 0, cols], result[0][:, cols])
+        for t in range(1, PACK):
             gate = sb("gate%d" % t, [P, S], F32)
-            result = sb("result%d" % t, [P, S], F32)
-            for half in range(2):
-                cols = slice(half * HALF, (half + 1) * HALF)
-                list_cols = slice(half * HALF // 16, (half + 1) * HALF // 16)
-                nc.scalar.activation(gate[:, cols], h_rows[t][:].indirect(lists["n3"][:, list_cols]), ACT.Sigmoid)
-                nc.vector.tensor_tensor(result[:, cols], hidden[t][:, cols], gate[:, cols], ALU.mult)
-                nc.sync.dma_start(out_rows[:, t, cols], result[:, cols])
+            edges = (0, HALF, S) if t < PACK - 1 else (0, HALF, HALF + QUARTER, S)
+            for lo, hi in zip(edges, edges[1:]):
+                nc.scalar.activation(gate[:, lo:hi], h_rows[t][:].indirect(entries("n3", lo, hi)), ACT.Sigmoid)
+                nc.vector.tensor_tensor(result[t][:, lo:hi], hidden[t][:, lo:hi], gate[:, lo:hi], ALU.mult)
+                nc.sync.dma_start(out_rows[:, t, lo:hi], result[t][:, lo:hi])

from contextlib import ExitStack

import concourse.mybir as mybir
from concourse.masks import make_identity

F32 = mybir.dt.float32
BF16 = mybir.dt.bfloat16
I32 = mybir.dt.int32
U32 = mybir.dt.uint32
U16 = mybir.dt.uint16
U8 = mybir.dt.uint8
FP8X4 = mybir.dt.float8_e4m3fn_x4
ACT = mybir.ActivationFunctionType
ALU = mybir.AluOpType

P = 128
PACK = 4
TABLE = 2048
S = 512
HALF = S // 2
QUARTER = S // 4
LIST = 16

FLOPS = 2 * 2 * 512 * 512 * 512

MU = 0.3125
WINDOW = -5.0 / 3.0
DIFF_SCALE = 0.5**0.5 / WINDOW
REST_SCALE = (1.0 - 2.0 * MU) * 0.5**0.5 / WINDOW


def tile_picked_keystdgate_none_p_kernel(
    tc, x_words, x_scales, d_words, d_scales, gn, w1, offs, kidx, n1, n2, n3, out
):
    nc = tc.nc
    with ExitStack() as ctx:
        keep = ctx.enter_context(tc.tile_pool(name="keep", bufs=1))
        psum = ctx.enter_context(tc.psum_pool(name="psum", bufs=1))

        def sb(name, shape, dtype, tag=None):
            return keep.tile(shape, dtype, name=name, tag=tag or name, align_bytes=64)

        lists = {}
        for name in ("kidx", "offs", "n1", "n2", "n3"):
            lists[name] = keep.tile([P, S // LIST], U16, name="list_" + name)

        def entries(name, lo, hi):
            return lists[name][:, lo // LIST : hi // LIST]

        d_scale_table = sb("d_scale_table", [P, TABLE], U8)
        x_scale_table = sb("x_scale_table", [P, TABLE], U8)
        nc.vector.memset(d_scale_table[:].bitcast(I32), 0)
        nc.gpsimd.memset(x_scale_table[:].bitcast(I32), 0)

        for name, source in (("kidx", kidx), ("offs", offs), ("n1", n1), ("n2", n2), ("n3", n3)):
            nc.sync.dma_start(lists[name][:], source)
        for j in range(2):
            nc.sync.dma_start(d_scale_table[j:P:16, :].bitcast(I32), d_scales[0][j:16:2, :].bitcast(I32))
        for q in range(4):
            nc.sync.dma_start(
                x_scale_table[32 * q : 32 * q + 4, :].bitcast(I32), x_scales[0][4 * q : 4 * q + 4, :].bitcast(I32)
            )

        warm_in = sb("warm_in", [P, 1], F32, tag="d_word_table")
        warm_out = sb("warm_out", [P, 1], F32, tag="x_word_table")
        nc.vector.memset(warm_in[:], 1.0)
        nc.scalar.activation(warm_out[:], warm_in[:], ACT.Abs_reciprocal_sqrt)
        d_word_table = sb("d_word_table", [P, TABLE], U32)
        x_word_table = sb("x_word_table", [P, TABLE], U32)
        nc.scalar.dma_start(d_word_table[:].bitcast(I32), d_words[0].rearrange("p n t -> p (n t)").bitcast(I32))
        nc.scalar.dma_start(x_word_table[:].bitcast(I32), x_words[0].rearrange("p n t -> p (n t)").bitcast(I32))

        identity = sb("identity", [P, P], F32)
        make_identity(nc, identity[:])

        d_scale_picked = sb("d_scale_picked", [P, S], U8, tag="d_picked")
        nc.vector.tensor_copy(d_scale_picked[:], d_scale_table[:].indirect(lists["kidx"][:]))
        key_scales = sb("key_scales", [P, S], U8)
        nc.vector.tensor_copy(
            key_scales[:].rearrange("p (t m) -> p m t", t=PACK), d_scale_picked[:].rearrange("p (m t) -> p m t", t=PACK)
        )
        for j in range(2):
            nc.sync.dma_start(key_scales[2 + j : P : 32, :].bitcast(I32), key_scales[16 + j : P : 32, :].bitcast(I32))
        gain = sb("gain", [P, PACK], F32, tag="d_scale_table")
        nc.sync.dma_start(gain[:], gn.rearrange("(p t) o -> p (t o)", t=PACK))
        query_scales = sb("query_scales", [P, S], U8)
        nc.vector.tensor_copy(query_scales[:], x_scale_table[:].indirect(lists["offs"][:]))
        d_word_picked = sb("d_word_picked", [P, S], U32, tag="d_picked")
        nc.vector.tensor_copy(d_word_picked[:], d_word_table[:].indirect(lists["kidx"][:]))
        key_words = sb("key_words", [P, S], U32)
        nc.vector.tensor_copy(
            key_words[:].bitcast(I32).rearrange("p (t m) -> p m t", t=PACK),
            d_word_picked[:].bitcast(I32).rearrange("p (m t) -> p m t", t=PACK),
        )
        w_raw = sb("w_raw", [P, PACK, S], F32, tag="d_word_table")
        nc.sync.dma_start(w_raw[:], w1.rearrange("(p j) n -> p j n", j=PACK))
        query_words = sb("query_words", [P, S], U32, tag="x_scale_table")
        for lo in (0, HALF):
            nc.vector.tensor_copy(query_words[:, lo : lo + HALF], x_word_table[:].indirect(entries("offs", lo, lo + HALF)))

        gain_self = sb("gain_self", [P, PACK], F32)
        gain_pair = sb("gain_pair", [P, PACK], F32)
        nc.vector.tensor_scalar(gain_pair[:], gain[:], -MU / WINDOW, None, ALU.mult)
        nc.vector.tensor_scalar(gain_self[:], gain[:], (1.0 - MU) / WINDOW, None, ALU.mult)

        window = []
        for t in range(PACK):
            scores = psum.tile([P, S], F32, name="scores", tag="row%d" % t)
            keys = slice(t * P, (t + 1) * P)
            window.append(sb("window%d" % t, [P, S], F32))
            for cols in (slice(0, HALF), slice(HALF, S)) if t == 0 else (slice(0, S),):
                nc.tensor.matmul_mx(
                    out=scores[:, cols],
                    lhsT=key_words[:, keys].bitcast(FP8X4),
                    lhsT_scale=key_scales[:, keys],
                    rhs=query_words[:, cols].bitcast(FP8X4),
                    rhs_scale=query_scales[:, cols],
                    start=True,
                    stop=True,
                )
                nc.scalar.activation(window[t][:, cols], scores[:, cols], ACT.Copy, scale=0.0625 * WINDOW)

        shifted = sb("shifted", [P, 2, S], F32)
        for t in range(2):
            nc.scalar.activation(shifted[:, t, :], window[t][:], ACT.Copy, scale=WINDOW)

        w_words = sb("w_words", [P, S], U32)
        w_scales = sb("w_scales", [P, S], U8)

        def halves(name):
            return [sb("%s%d" % (name, h), [P, PACK, HALF], F32) for h in range(2)]

        pair_sum, inv_root, top = (halves(name) for name in ("pair_sum", "inv_root", "top"))
        self_term, w_grouped, diff_sq, rest_sq, spread, hidden = [], [], [], [], [], []

        def turn(bank, b, source, start=False, stop=False):
            nc.tensor.matmul(bank[:, b, :], source, identity[:], start=start, stop=stop, is_transpose=True)

        def block(rows, b):
            return rows[:, b // 2, (b % 2) * P : (b % 2 + 1) * P]

        def gather(u):
            h, t0 = u % 2, 2 * (u // 2)
            lo, hi = h * HALF, (h + 1) * HALF
            pa_neg = sb("pa_neg%d" % u, [P, 2, HALF], F32)
            both = pair_sum[h][:, t0 : t0 + 2, :]
            for i in range(2):
                nc.vector.tensor_scalar(
                    pa_neg[:, i, :], window[t0 + i][:].indirect(entries("n1", lo, hi)), -1.0, 0.0, ALU.mult, ALU.add
                )
            for i in range(2):
                nc.vector.tensor_tensor(
                    both[:, i, :], window[t0 + i][:].indirect(entries("n2", lo, hi)), pa_neg[:, i, :], ALU.subtract
                )
            return pa_neg, both

        def turned_squares(u, pa_neg, both):
            diff_t = psum.tile([P, 4, P], F32, name="diff_t", tag="diff_t%d" % u)
            for twice in range(2):
                for b in range(4):
                    turn(diff_t, b, block(pa_neg, b), start=(twice == 0 and b == 0))
            for b in range(4):
                turn(diff_t, b, block(both, b), stop=(b == 3))
            diff_sq.append(sb("diff_sq%d" % u, [P, 4, P], F32))
            nc.scalar.activation(diff_sq[u][:], diff_t[:], ACT.Square, scale=DIFF_SCALE)
            rest_t = psum.tile([P, 4, P], F32, name="rest_t", tag="rest_t%d" % u)
            for b in range(4):
                turn(rest_t, b, block(both, b), start=(b == 0))
            for b in range(4):
                turn(rest_t, b, block(shifted[:, :, u * HALF : (u + 1) * HALF], b), stop=(b == 3))
            rest_sq.append(sb("rest_sq%d" % u, [P, 4, P], F32))
            nc.scalar.activation(rest_sq[u][:], rest_t[:], ACT.Square, scale=REST_SCALE)
            spread.append(psum.tile([P, 4, P], F32, name="spread", tag="diff_t%d" % u))
            for b in range(4):
                turn(spread[u], b, diff_sq[u][:, b, :], start=(b == 0))

        def turned_root(u):
            for b in range(4):
                turn(spread[u], b, rest_sq[u][:, b, :], stop=(b == 3))
            nc.scalar.activation(
                inv_root[u][:, 0:2, :].rearrange("p t n -> p (t n)"),
                spread[u][:].rearrange("p b n -> p (b n)"),
                ACT.Abs_reciprocal_sqrt,
                bias=0.25,
            )

        def plain_squares(u, pa_neg, both, rest_out, diff_out):
            h = u % 2
            rest = sb("rest%d" % u, [P, 2, HALF], F32)
            for i in range(2):
                nc.vector.scalar_tensor_tensor(
                    rest[:, i, :], window[2 + i][:, h * HALF : (h + 1) * HALF], WINDOW, both[:, i, :], ALU.mult, ALU.add
                )
            rest_sq.append(rest_out)
            diff_sq.append(diff_out)
            nc.scalar.activation(rest_out, rest[:], ACT.Square, scale=REST_SCALE)
            diff = sb("diff%d" % u, [P, 2, HALF], F32)
            nc.vector.scalar_tensor_tensor(diff[:], pa_neg[:], 2.0, both, ALU.mult, ALU.add)
            nc.scalar.activation(diff_out, diff[:], ACT.Square, scale=DIFF_SCALE)

        def plain_root(u):
            squares = sb("squares%d" % u, [P, 2, HALF], F32)
            nc.vector.tensor_tensor(squares[:], diff_sq[u], rest_sq[u], ALU.add)
            nc.scalar.activation(inv_root[u % 2][:, 2:4, :], squares[:], ACT.Abs_reciprocal_sqrt, bias=0.25)

        def group_weights(i, tag):
            w_grouped.append(sb("w_grouped%d" % i, [P, 2 * S], BF16, tag=tag))
            nc.scalar.copy(
                w_grouped[i][:].rearrange("p (t m j) -> p m j t", t=2, j=PACK),
                w_raw[:].rearrange("p j (m t) -> p m j t", t=PACK)[:, :, :, 2 * i : 2 * i + 2],
            )

        h_rows = [sb("h_rows%d" % t, [P, S], F32) for t in range(PACK)]

        def top_half(h):
            for t in range(PACK):
                nc.vector.scalar_tensor_tensor(
                    top[h][:, t, :],
                    pair_sum[h][:, t, :],
                    gain_pair[:, t : t + 1],
                    self_term[t][:, h * HALF : (h + 1) * HALF],
                    ALU.mult,
                    ALU.add,
                )

        def divide(h, lo, width):
            z = sb("z%d_%d" % (h, lo), [P, width * PACK], BF16)
            nc.vector.tensor_tensor(
                z[:].rearrange("p (g i t) -> p g t i", i=4, t=PACK),
                top[h][:, :, lo : lo + width].rearrange("p t (g i) -> p g t i", i=4),
                inv_root[h][:, :, lo : lo + width].rearrange("p t (g i) -> p g t i", i=4),
                ALU.mult,
            )
            return z

        def quantise(z, name, width):
            z_words = sb("z_words" + name, [P, width], U32)
            z_scales = sb("z_scales" + name, [P, width], U8)
            nc.vector.quantize_mx(out=z_words[:].bitcast(FP8X4), scales=z_scales[:], in_=z[:])
            return z_words, z_scales

        def second_product(t, codes, lo, width):
            rows = slice(t * P, (t + 1) * P)
            nc.tensor.matmul_mx(
                out=hidden[t][:, lo : lo + width],
                lhsT=w_words[:, rows].bitcast(FP8X4),
                lhsT_scale=w_scales[:, rows],
                rhs=codes[0][:].bitcast(FP8X4),
                rhs_scale=codes[1][:],
                start=True,
                stop=True,
            )

        turned_squares(0, *gather(0))
        for t in range(PACK):
            self_term.append(sb("self_term%d" % t, [P, S], F32))
            nc.scalar.activation(self_term[t][:], window[t][:], ACT.Copy, scale=gain_self[:, t : t + 1])
        picked = gather(1)
        turned_root(0)
        turned_squares(1, *picked)
        group_weights(0, "diff_sq0")
        group_weights(1, "rest_sq0")
        picked = gather(2)
        turned_root(1)
        both_sq = sb("both_sq", [P, 2, 2, HALF], F32, tag="d_word_table")
        plain_squares(2, *picked, both_sq[:, 0], both_sq[:, 1])
        picked = gather(3)
        rest_sq_last = sb("rest_sq3", [P, 2, HALF], F32, tag="rest2")
        diff_sq_last = sb("diff_sq3", [P, 2, HALF], F32, tag="diff2")
        plain_squares(3, *picked, rest_sq_last[:], diff_sq_last[:])
        plain_root(2)
        for t in range(PACK):
            hidden.append(psum.tile([P, S], F32, name="hidden", tag="row%d" % t))
        top_half(0)
        plain_root(3)
        warm_gate = sb("warm_gate", [P, 1], F32)
        nc.scalar.activation(warm_gate[:], inv_root[1][:, PACK - 1, 0:1], ACT.Sigmoid)
        for i in range(2):
            cols = slice(i * HALF, (i + 1) * HALF)
            nc.vector.quantize_mx(out=w_words[:, cols].bitcast(FP8X4), scales=w_scales[:, cols], in_=w_grouped[i][:])
        z_first = divide(0, 0, HALF)
        top_half(1)
        codes_first = quantise(z_first, "_first", HALF)
        for t in range(PACK):
            second_product(t, codes_first, 0, HALF)

        gate_rows = sb("gate_rows", [P, S], F32)
        for t in range(PACK):
            nc.scalar.copy(h_rows[t][:, 0:HALF], hidden[t][:, 0:HALF])
        nc.scalar.activation(gate_rows[:, 0:HALF], hidden[0][:, 0:HALF], ACT.Sigmoid)
        z_third = divide(1, 0, QUARTER)
        z_last = divide(1, QUARTER, QUARTER)
        codes_third = quantise(z_third, "_third", QUARTER)
        codes_last = quantise(z_last, "_last", QUARTER)
        for t in range(PACK):
            second_product(t, codes_third, HALF, QUARTER)
            second_product(t, codes_last, HALF + QUARTER, QUARTER)
        nc.scalar.activation(gate_rows[:, HALF:S], hidden[0][:, HALF:S], ACT.Sigmoid)
        nc.scalar.copy(h_rows[0][:, HALF:S], hidden[0][:, HALF:S])
        for t in range(1, PACK):
            nc.vector.tensor_copy(h_rows[t][:, HALF:S], hidden[t][:, HALF:S])

        out_rows = out.rearrange("(p t) n -> p t n", t=PACK)
        result = [sb("result%d" % t, [P, S], F32) for t in range(PACK)]
        for lo in (0, HALF):
            cols = slice(lo, lo + HALF)
            nc.vector.tensor_tensor(
                result[0][:, cols], gate_rows[:].indirect(entries("n3", lo, lo + HALF)), h_rows[0][:, cols], ALU.mult
            )
            nc.sync.dma_start(out_rows[:, 0, cols], result[0][:, cols])
        for t in range(1, PACK):
            gate = sb("gate%d" % t, [P, S], F32)
            edges = (0, HALF, S) if t < PACK - 1 else (0, HALF, HALF + QUARTER, S)
            for lo, hi in zip(edges, edges[1:]):
                nc.scalar.activation(gate[:, lo:hi], h_rows[t][:].indirect(entries("n3", lo, hi)), ACT.Sigmoid)
                nc.vector.tensor_tensor(result[t][:, lo:hi], hidden[t][:, lo:hi], gate[:, lo:hi], ALU.mult)
                nc.sync.dma_start(out_rows[:, t, lo:hi], result[t][:, lo:hi])
